import numpy as np, ml_dtypes
CORES = [23,119,17,113]
N = 4
import mx_ref
NC, HD, G = 256, 2, 4
C, DEC = np.float32(0.023), np.float32(0.8)
BF = ml_dtypes.bfloat16
def cut(t, i, w=512):
    return t[:, w * i:w * i + w]
def tile(rs):
    return np.stack(rs, axis=2).reshape(128, -1).astype(BF)
def layer(w, X):
    out = []
    for i in range(G):
        for t in range(len(X)):
            p = mx_ref.matmul(mx_ref.quantize(cut(w, len(X) * i + t)), X[t])
            z = p if t == 0 else z + p
        out.append(z)
    return out
def pick(b):
    s = np.zeros((128, 128, 4), np.float32)
    s[np.arange(128), np.arange(128), b] = 1.0
    return mx_ref.quantize(s.reshape(128, 512).astype(BF))
def setup_inputs(rng):
    def f(*shape):
        return mx_ref.flush((rng.standard_normal(shape, dtype=np.float32) * np.exp2(rng.integers(-2, 3, shape[:-1] + (1,)))).astype(BF))
    return {"k": f(N, 128, HD * 4 * 512), "v": f(N, 128, HD * 512), "q": f(N, 128, HD * 4 * NC)}
def setup_inputs_blocks(rng):
    d = setup_inputs(rng)
    for k in ("k", "v", "q"): d[k] = mx_ref.spread(d[k], rng, 4)
    return d
def setup_inputs_wide(rng):
    d = setup_inputs(rng)
    for k in ("k", "v", "q"): d[k] = mx_ref.flush((d[k].astype(np.float32) * np.exp2(rng.integers(-4, 5, (N, 1, 1))).astype(np.float32)).astype(BF))
    return d
def setup_inputs_zeros(rng):
    d = setup_inputs(rng); v = d["v"].reshape(N, 128, -1, 4).copy()
    v[np.broadcast_to((rng.random((N, 1, v.shape[2], 1)) < 0.33), v.shape)] = 0
    d["v"] = v.reshape(d["v"].shape)
    return d
def reference(k, v, q):
    S = [pick(t) for t in range(4)]
    y = np.zeros((N, 128, HD * NC), np.float32)
    for a in range(HD):
        for r in range(N):
            R = [z * C for z in layer(cut(k[r], a, 4 * 512), [mx_ref.quantize(cut(v[r], a))])]
            if r > 0: R = [R[t] + mx_ref.matmul(S[t], s) * DEC for t in range(4)]
            s = mx_ref.quantize(tile(R))
            y[r][:, NC * a:NC * a + NC] = mx_ref.matmul(s, mx_ref.quantize(cut(q[r], a, 4 * NC)))
    return {"y": y}

import numpy as np
from concourse.mybir import dt, AluOpType, ActivationFunctionType

HD, G, W, NC = 2, 4, 128, 256
C, DEC = float(np.float32(0.023)), float(np.float32(0.8))
F8 = "float8_e4m3fn_x4"

SCRATCH = {
    "kb": ("sbuf", [128, HD * G * 4 * W], "bfloat16"), "kq": ("sbuf", [128, HD * G * W], F8), "ks": ("sbuf", [128, HD * G * W], "uint8"),
    "vb": ("sbuf", [128, HD * 4 * W], "bfloat16"), "vq": ("sbuf", [128, HD * W], F8), "vs": ("sbuf", [128, HD * W], "uint8"),
    "qb": ("sbuf", [128, HD * 4 * NC], "bfloat16"), "qq": ("sbuf", [128, HD * NC], F8), "qs": ("sbuf", [128, HD * NC], "uint8"),
    "ones": ("sbuf", [128, 4 * W + 4], "bfloat16"), "eye": ("sbuf", [128, 4 * W + 4], "bfloat16"),
    "pq": ("sbuf", [128, G * W], F8), "ps": ("sbuf", [128, G * W], "uint8"),
    "zc": ("sbuf", [128, HD * G * W], "float32"), "dc": ("sbuf", [128, HD * G * W], "float32"),
    "yb": ("sbuf", [128, HD * NC], "float32"),
    "acc": ("psum", [128, 512 * HD * G], "float32"),
}
for _a in range(HD):
    SCRATCH["t%d" % _a] = ("sbuf", [128, 4 * W], "bfloat16")
    SCRATCH["oq%d" % _a] = ("sbuf", [128, W], F8)
    SCRATCH["os%d" % _a] = ("sbuf", [128, W], "uint8")
    SCRATCH["iq%d" % _a] = ("sbuf", [128, W], F8)
    SCRATCH["is%d" % _a] = ("sbuf", [128, W], "uint8")

KPARTS = [(0, 2), (2, 2), (4, 2), (6, 1), (7, 1)]

SEMAPHORES = (["lv", "lq", "qv", "qqd", "ones", "eye", "pd", "st"]
              + ["lk%d" % i for i in range(len(KPARTS))] + ["qk%d" % i for i in range(len(KPARTS))]
              + ["%s%d" % (s, a) for s in ("arr", "sent", "zs", "ad", "sq", "yd", "yv", "yc") for a in range(HD)]
              + ["%s%d%d" % (s, a, b) for s in ("z", "d", "m") for a in range(HD) for b in range(G)])


def rank_program(g, core, T, topo):
    rank = T.rank_of(core)
    if rank is None:
        return
    sem, last = T.sem, rank == len(T.cores) - 1
    copy = ActivationFunctionType.Copy

    def bank(a, b, n=W):
        c = 512 * (G * a + b)
        return T.acc[:, c:c + n]

    def col(t, i, n=1, w=W):
        return t[:, w * i:w * (i + n)]

    def load_k(queue, i):
        t0, n = KPARTS[i]
        queue.dma_start(col(T.kb, t0, n, 4 * W), col(T.k, t0, n, 4 * W)).then_inc(sem["lk%d" % i], 16)

    g.sync.dma_start(T.vb[:], T.v[:]).then_inc(sem.lv, 16)
    for i in range(len(KPARTS)):
        load_k(g.scalar if i % 2 == 0 else g.sync, i)
    if rank == 0:
        g.sync.wait_ge(sem.sent1, SENT(topo, T, rank))
    g.sync.dma_start(T.qb[:], T.q[:]).then_inc(sem.lq, 16)

    if rank > 0:
        g.vector.memset(T.ones[:], 1.0).then_inc(sem.ones, 1)
        g.wait_ge(sem.ones, 1)
        g.affine_select(T.eye[:], T.ones[:], [[-1, 4 * W + 4]], AluOpType.is_equal, 0.0, 3, 4).then_inc(sem.eye, 1)
        g.vector.wait_ge(sem.eye, 1)
        for b in range(G):
            g.vector.quantize_mx(col(T.pq, b), col(T.ps, b), T.eye[:, 3 - b:3 - b + 4 * W]).then_inc(sem.pd, 1)

    def quant_q():
        g.vector.wait_ge(sem.lq, 16)
        g.vector.quantize_mx(T.qq[:], T.qs[:], T.qb[:]).then_inc(sem.qqd, 1)

    def quant_state(a, s, n):
        g.vector.wait_ge(s, n)
        g.vector.quantize_mx(T["oq%d" % a][:], T["os%d" % a][:], T["t%d" % a][:]).then_inc(sem["sq%d" % a], 1)

    g.vector.wait_ge(sem.lv, 16)
    g.vector.quantize_mx(T.vq[:], T.vs[:], T.vb[:]).then_inc(sem.qv, 1)
    for i, (t0, n) in enumerate(KPARTS):
        g.vector.wait_ge(sem["lk%d" % i], 16)
        g.vector.quantize_mx(col(T.kq, t0, n), col(T.ks, t0, n), col(T.kb, t0, n, 4 * W)).then_inc(sem["qk%d" % i], 1)
        if rank == 0 and (t0 + n) % G == 0:
            quant_state(t0 // G, sem["zs%d" % (t0 // G)], G)

    g.tensor.wait_ge(sem.qv, 1)
    for i, (t0, n) in enumerate(KPARTS):
        g.tensor.wait_ge(sem["qk%d" % i], 1)
        for t in range(t0, t0 + n):
            a, b = divmod(t, G)
            g.tensor.matmul_mx(bank(a, b), col(T.kq, t), col(T.ks, t), col(T.vq, a), col(T.vs, a), True, True).then_inc(sem["z%d%d" % (a, b)], 1)
            g.scalar.wait_ge(sem["z%d%d" % (a, b)], 1)
            out = T["t%d" % a][:, b:4 * W:4] if rank == 0 else col(T.zc, t)
            g.scalar.activation(out, bank(a, b), copy, scale=C).then_inc(sem["zs%d" % a], 1)

    if rank > 0:
        if last:
            quant_q()
        g.tensor.wait_ge(sem.pd, G)
        for a in range(HD):
            g.tensor.wait_ge(sem["zs%d" % a], G)
            g.tensor.wait_ge(sem["arr%d" % a], SENT(topo, T, rank - 1))
            if a == 0:
                g.vector.wait_ge(sem.zs1, G)
                g.vector.wait_ge(sem.zs0, G)
            for b in range(G):
                i = G * a + b
                g.tensor.matmul_mx(bank(a, b), col(T.pq, b), col(T.ps, b), T["iq%d" % a][:], T["is%d" % a][:], True, True).then_inc(sem["d%d%d" % (a, b)], 1)
                g.scalar.wait_ge(sem["d%d%d" % (a, b)], 1)
                g.scalar.activation(col(T.dc, i), bank(a, b), copy, scale=DEC).then_inc(sem["m%d%d" % (a, b)], 1)
                g.vector.wait_ge(sem["m%d%d" % (a, b)], 1)
                g.vector.tensor_tensor(T["t%d" % a][:, b:4 * W:4], col(T.zc, i), col(T.dc, i), AluOpType.add).then_inc(sem["ad%d" % a], 1)
            quant_state(a, sem["ad%d" % a], G)
    if not last:
        quant_q()

    if not last:
        dst = T.cores[rank + 1]
        rid, pid, _ = topo.addr(dst)
        mask = topo.mask(core, dst)
        for a in range(HD):
            g.wait_ge(sem["sq%d" % a], 1)
            g.remote_dma(T["iq%d" % a][:].bitcast(dt.uint8), T["oq%d" % a][:].bitcast(dt.uint8), sem["arr%d" % a], sem["sent%d" % a], pid, rid, mask)
            g.remote_dma(T["is%d" % a][:], T["os%d" % a][:], sem["arr%d" % a], sem["sent%d" % a], pid, rid, mask)
        for a in range(HD):
            g.wait_ge(sem["sent%d" % a], SENT(topo, T, rank))

    g.tensor.wait_ge(sem.sq0, 1)
    g.tensor.wait_ge(sem.qqd, 1)
    g.tensor.matmul_mx(bank(0, 0, NC), T.oq0[:], T.os0[:], col(T.qq, 0, 2), col(T.qs, 0, 2), True, True).then_inc(sem.yd0, 1)
    g.scalar.wait_ge(sem.yd0, 1)
    g.scalar.activation(T.yb[:, 0:NC], bank(0, 0, NC), copy).then_inc(sem.yc0, 1)
    g.tensor.wait_ge(sem.sq1, 1)
    g.tensor.matmul_mx(bank(0, 1), T.oq1[:], T.os1[:], col(T.qq, 2), col(T.qs, 2), True, True).then_inc(sem.yv0, 1)
    g.tensor.matmul_mx(bank(0, 2), T.oq1[:], T.os1[:], col(T.qq, 3), col(T.qs, 3), True, True).then_inc(sem.yd1, 1)
    g.vector.wait_ge(sem.yv0, 1)
    g.vector.tensor_copy(col(T.yb, 2), bank(0, 1)).then_inc(sem.yv1, 1)
    g.scalar.wait_ge(sem.yd1, 1)
    g.scalar.activation(col(T.yb, 3), bank(0, 2), copy).then_inc(sem.yc1, 1)
    if last:
        g.sync.wait_ge(sem.yc0, 1)
        g.sync.dma_start(T.y[:, 0:NC], T.yb[:, 0:NC]).then_inc(sem.st, 16)
        g.sync.wait_ge(sem.yv1, 1)
        g.sync.wait_ge(sem.yc1, 1)
        g.sync.dma_start(T.y[:, NC:2 * NC], T.yb[:, NC:2 * NC]).then_inc(sem.st, 16)
        g.sync.wait_ge(sem.st, 32)
    else:
        g.sync.wait_ge(sem.sent1, SENT(topo, T, rank))
        g.sync.wait_ge(sem.yc0, 1)
        g.sync.wait_ge(sem.yv1, 1)
        g.sync.wait_ge(sem.yc1, 1)
        g.sync.dma_start(T.y[:], T.yb[:]).then_inc(sem.st, 16)
        g.sync.wait_ge(sem.st, 16)


def SENT(topo, T, r):
    return 2 * bin(topo.mask(T.cores[r], T.cores[r + 1])).count("1")
